import numpy as np
import ml_dtypes


def mxq(x, axis, fmt="e4m3"):
    dtype, down = {"e4m3": (ml_dtypes.float8_e4m3fn, 7), "e5m2": (ml_dtypes.float8_e5m2, 14)}[fmt]
    v = np.moveaxis(np.asarray(x, np.float32).astype(ml_dtypes.bfloat16).astype(np.float64), axis, -1)
    blocks = v.reshape(v.shape[:-1] + (-1, 32))
    amax = np.abs(blocks).max(-1, keepdims=True)
    byte = np.maximum(np.where(amax > 0, np.frexp(amax)[1] - 1 + 127, 0) - down, 1)
    scale = np.exp2(byte - 127.0)
    codes = (blocks / scale).astype(np.float32).astype(dtype).astype(np.float64)
    return np.moveaxis((codes * scale).reshape(v.shape), -1, axis)


WIDE = False


def mx_kscale(k):
    if not WIDE:
        return np.ones(k)
    levels = np.array([10, -10, 5, -5, 0])
    if k % 512:
        return np.exp2(np.random.permutation(np.resize(levels, k // 32))).repeat(32)
    a = np.empty((k // 512, 16))
    for p in range(k // 512):
        a[p, :8] = np.random.permutation(np.resize(levels, 8))
        for g in range(8):
            far = levels[np.abs(levels - a[p, g]) >= 10]
            a[p, g + 8] = far[np.random.randint(len(far))]
    return np.exp2(a.ravel()).repeat(32)


def f64(x):
    return np.asarray(x).astype(np.float64)


def striped(idx):
    return np.tile(idx.reshape(-1, 16).T, (8, 1)).astype(np.uint16)


def unstriped(offs):
    return offs[:16].T.reshape(-1).astype(np.int64)


def pack_weight(w):
    k, n = w.shape
    w = f64(np.asarray(w, np.float32).astype(ml_dtypes.bfloat16)).reshape(k // 32, 32, n)
    amax = np.abs(w).max(1)
    byte = np.clip(np.where(amax > 0, np.frexp(amax)[1] - 1 + 127 - 7, 1), 1, 254)
    scaled = (w * np.exp2(127.0 - byte)[:, None, :]).reshape(k, n).astype(np.float32)
    words = np.ascontiguousarray(scaled.reshape(k // 512, 128, 4, n).transpose(0, 1, 3, 2)).astype(ml_dtypes.float8_e4m3fn).view(np.uint8)
    return words, np.ascontiguousarray(byte.astype(np.uint8).reshape(k // 512, 16, n))


def unpack_weight(words, scales):
    g, p, n, _ = words.shape
    vals = np.ascontiguousarray(words).view(ml_dtypes.float8_e4m3fn).astype(np.float64) * np.repeat(np.exp2(scales.astype(np.float64) - 127.0), 8, axis=1)[..., None]
    return vals.transpose(0, 1, 3, 2).reshape(g * 512, n)


def relu(v):
    return np.maximum(v, 0.0)


K, T, E, C, N = 1536, 512, 2, 256, 512


def by_expert(wq, xq):
    return np.concatenate([wq[e].T @ xq[:, e * C:(e + 1) * C] for e in range(E)], axis=1)


def setup_inputs():
    n = np.random.standard_normal
    s = mx_kscale(K)[:, None]
    packed = [pack_weight(m) for m in n((E, K, N)) / np.sqrt(K) / s[None]]
    return {
        "xT": (n((K, T)) * s).astype(np.float32),
        "w_words": np.stack([m[0] for m in packed]),
        "w_scales": np.stack([m[1] for m in packed]),
        "b": (0.3 * n((N, E))).astype(np.float32),
        "gate": np.tile(np.random.uniform(0.2, 1.0, E * C), (N, 1)).astype(np.float32),
        "offs": striped(np.random.permutation(T)[:E * C]),
    }


def reference(xT, w_words, w_scales, b, gate, offs):
    idx = unstriped(offs)
    xq = mxq(f64(xT)[:, idx], 0, "e4m3")
    w = np.stack([unpack_weight(w_words[e], w_scales[e]) for e in range(E)])
    y = by_expert(w, xq)
    y = relu(y + np.repeat(f64(b), C, axis=1))
    out = np.zeros((N, T))
    out[:, idx] = f64(gate) * y
    return out

@@ -1,0 +1,110 @@
+from contextlib import ExitStack
+
+import concourse.mybir as mybir
+
+K, T, E, C, N = 1536, 512, 2, 256, 512
+P = 128
+PACK = 4
+K_PASS = P * PACK
+PASSES = K // K_PASS
+BLOCKS = N // P
+QUADS = 4
+
+FLOPS = 2 * K * E * C * N
+BYTES = 4 * K * T + E * K * N + E * (K // 32) * N + 4 * N * E + 4 * E * C + 2 * E * C + 4 * N * T
+
+F32 = mybir.dt.float32
+BF16 = mybir.dt.bfloat16
+I32 = mybir.dt.int32
+U32 = mybir.dt.uint32
+U16 = mybir.dt.uint16
+U8 = mybir.dt.uint8
+FP8X4 = mybir.dt.float8_e4m3fn_x4
+COPY = mybir.ActivationFunctionType.Copy
+RELU = mybir.ActivationFunctionType.Relu
+MULT = mybir.AluOpType.mult
+
+
+def tile_routed_moe_kernel(tc, xT, w_words, w_scales, b, gate, offs, out):
+    nc = tc.nc
+    with ExitStack() as ctx:
+        keep = ctx.enter_context(tc.tile_pool(name="keep", bufs=1))
+        psum = ctx.enter_context(tc.psum_pool(name="psum", bufs=1))
+
+        offsets = keep.tile([P, T // 16], U16, name="offsets")
+        nc.sync.dma_start(offsets[:], offs)
+
+        token_bytes = keep.tile([P, T], U8, name="token_bytes", align_bytes=64)
+        nc.gpsimd.memset(token_bytes[:], 0)
+        w_bytes = keep.tile([P, E * PASSES, N], U8, name="w_bytes", align_bytes=64)
+        nc.vector.memset(w_bytes[:].rearrange("p a n -> p (a n)").bitcast(I32), 0)
+        bias = keep.tile([P, BLOCKS, E], F32, name="bias")
+        nc.scalar.dma_start(bias[:], b.rearrange("(c p) e -> p c e", p=P))
+
+        x_rows = xT.rearrange("(a p j) t -> a p j t", p=P, j=PACK)
+        pieces = [(0, 0, 256, 80), (0, 256, 512, 336), (1, 0, 512, 160), (2, 0, 256, 96), (2, 256, 512, 368)]
+        raw = []
+        for a, t0, t1, ts in pieces:
+            r = keep.tile([P, PACK, t1 - t0], F32, name=f"raw{a}_{t0}")
+            nc.sync.dma_start(r[:], x_rows[a, :, :, t0:t1])
+            raw.append(r)
+
+        scale_rows = w_scales.rearrange("e a q n -> q (e a) n")
+        for q in range(QUADS):
+            nc.sync.dma_start(w_bytes[32 * q : 32 * q + 4, :, :].bitcast(I32), scale_rows[4 * q : 4 * q + 4, :, :].bitcast(I32))
+        w_codes = []
+        for e in range(E):
+            wc = keep.tile([P, PASSES, N], I32, name=f"w_codes{e}", align_bytes=64)
+            nc.sync.dma_start(wc[:], w_words[e].rearrange("a p n r -> p a (n r)").bitcast(I32))
+            w_codes.append(wc)
+        gate_rows = keep.tile([P, E * C], F32, name="gate_rows")
+        nc.sync.dma_start(gate_rows[:], gate[0:P, :])
+
+        grouped = [keep.tile([P, T, PACK], BF16, name=f"grouped{a}", align_bytes=64) for a in range(PASSES)]
+        token_words = [keep.tile([P, T], U32, name=f"token_words{a}", align_bytes=64) for a in range(PASSES)]
+        slot_words = [keep.tile([P, E * C], U32, name=f"slot_words{a}", align_bytes=64) for a in range(PASSES)]
+        slot_bytes = keep.tile([P, E * C], U8, name="slot_bytes", align_bytes=64)
+
+        def gather_words(a, e):
+            cols = slice(e * C, (e + 1) * C)
+            nc.vector.tensor_copy(slot_words[a][:, cols], token_words[a][:].indirect(offsets[:, e * C // 16 : (e + 1) * C // 16]))
+
+        for (a, t0, t1, ts), r in zip(pieces, raw):
+            nc.scalar.copy(grouped[a][:, ts:t1, :], r[:, :, ts - t0 : t1 - t0].rearrange("p j t -> p t j"))
+            nc.vector.tensor_copy(grouped[a][:, t0:ts, :], r[:, :, 0 : ts - t0].rearrange("p j t -> p t j"))
+            nc.vector.quantize_mx(
+                out=token_words[a][:, t0:t1].bitcast(FP8X4),
+                scales=token_bytes[4 * a : P, t0:t1],
+                in_=grouped[a][:, t0:t1, :].rearrange("p t j -> p (t j)"),
+            )
+            if a < PASSES - 1 and t1 == T:
+                for e in range(E):
+                    gather_words(a, e)
+        for e in range(E):
+            cols = slice(e * C, (e + 1) * C)
+            nc.vector.tensor_copy(slot_bytes[:, cols], token_bytes[:].indirect(offsets[:, e * C // 16 : (e + 1) * C // 16]))
+            gather_words(PASSES - 1, e)
+
+        windows = [keep.tile([P, T], F32, name=f"window{c}") for c in range(BLOCKS)]
+        for e in range(E):
+            cols = slice(e * C, (e + 1) * C)
+            for c in range(BLOCKS):
+                acc = psum.tile([P, C], F32, name=f"acc{e}_{c}")
+                feats = slice(c * P, (c + 1) * P)
+                for a in range(PASSES):
+                    nc.tensor.matmul_mx(
+                        out=acc[:],
+                        lhsT=w_codes[e][:, a, feats].bitcast(FP8X4),
+                        lhsT_scale=w_bytes[:, e * PASSES + a, feats],
+                        rhs=slot_words[a][:, cols].bitcast(FP8X4),
+                        rhs_scale=slot_bytes[4 * a : P, cols],
+                        start=(a == 0),
+                        stop=(a == PASSES - 1),
+                    )
+                y = keep.tile([P, C], F32, name=f"y{e}_{c}")
+                nc.scalar.activation(y[:], acc[:], RELU, bias=bias[:, c, e : e + 1])
+                z = keep.tile([P, C], F32, name=f"z{e}_{c}")
+                nc.gpsimd.tensor_tensor(z[:], y[:], gate_rows[:, cols], MULT)
+                nc.vector.tensor_copy(windows[c][:].indirect(offsets[:, e * C // 16 : (e + 1) * C // 16]), z[:])
+                if e == E - 1:
+                    nc.sync.dma_start(out[c * P : (c + 1) * P, :], windows[c][:])

@@ -31,23 +31,22 @@ def tile_routed_moe_kernel(tc, xT, w_words, w_scales, b, gate, offs, out):
         keep = ctx.enter_context(tc.tile_pool(name="keep", bufs=1))
         psum = ctx.enter_context(tc.psum_pool(name="psum", bufs=1))
 
-        offsets = keep.tile([P, T // 16], U16, name="offsets")
-        nc.sync.dma_start(offsets[:], offs)
-
         token_bytes = keep.tile([P, T], U8, name="token_bytes", align_bytes=64)
         nc.gpsimd.memset(token_bytes[:], 0)
         w_bytes = keep.tile([P, E * PASSES, N], U8, name="w_bytes", align_bytes=64)
         nc.vector.memset(w_bytes[:].rearrange("p a n -> p (a n)").bitcast(I32), 0)
         bias = keep.tile([P, BLOCKS, E], F32, name="bias")
-        nc.scalar.dma_start(bias[:], b.rearrange("(c p) e -> p c e", p=P))
 
         x_rows = xT.rearrange("(a p j) t -> a p j t", p=P, j=PACK)
-        pieces = [(0, 0, 256, 80), (0, 256, 512, 336), (1, 0, 512, 160), (2, 0, 256, 96), (2, 256, 512, 368)]
-        raw = []
-        for a, t0, t1, ts in pieces:
+        raw = {}
+        for a, t0, t1 in [(0, 0, 256), (0, 256, 512), (1, 0, 512), (2, 0, 384), (2, 384, 512)]:
             r = keep.tile([P, PACK, t1 - t0], F32, name=f"raw{a}_{t0}")
             nc.sync.dma_start(r[:], x_rows[a, :, :, t0:t1])
-            raw.append(r)
+            raw[(a, t0)] = r
+        pieces = [(0, 0, 256, 64, 0), (0, 256, 512, 320, 256), (1, 0, 512, 128, 0), (2, 0, 256, 64, 0), (2, 256, 384, 320, 0), (2, 384, 512, 448, 384)]
+
+        offsets = keep.tile([P, T // 16], U16, name="offsets")
+        nc.sync.dma_start(offsets[:], offs)
 
         scale_rows = w_scales.rearrange("e a q n -> q (e a) n")
         for q in range(QUADS):
@@ -57,8 +56,10 @@ def tile_routed_moe_kernel(tc, xT, w_words, w_scales, b, gate, offs, out):
             wc = keep.tile([P, PASSES, N], I32, name=f"w_codes{e}", align_bytes=64)
             nc.sync.dma_start(wc[:], w_words[e].rearrange("a p n r -> p a (n r)").bitcast(I32))
             w_codes.append(wc)
-        gate_rows = keep.tile([P, E * C], F32, name="gate_rows")
-        nc.sync.dma_start(gate_rows[:], gate[0:P, :])
+            if e == 0:
+                nc.sync.dma_start(bias[:], b.rearrange("(c p) e -> p c e", p=P))
+                gate_rows = keep.tile([P, E * C], F32, name="gate_rows")
+                nc.sync.dma_start(gate_rows[:], gate[0:P, :])
 
         grouped = [keep.tile([P, T, PACK], BF16, name=f"grouped{a}", align_bytes=64) for a in range(PASSES)]
         token_words = [keep.tile([P, T], U32, name=f"token_words{a}", align_bytes=64) for a in range(PASSES)]
@@ -69,9 +70,10 @@ def tile_routed_moe_kernel(tc, xT, w_words, w_scales, b, gate, offs, out):
             cols = slice(e * C, (e + 1) * C)
             nc.vector.tensor_copy(slot_words[a][:, cols], token_words[a][:].indirect(offsets[:, e * C // 16 : (e + 1) * C // 16]))
 
-        for (a, t0, t1, ts), r in zip(pieces, raw):
-            nc.scalar.copy(grouped[a][:, ts:t1, :], r[:, :, ts - t0 : t1 - t0].rearrange("p j t -> p t j"))
-            nc.vector.tensor_copy(grouped[a][:, t0:ts, :], r[:, :, 0 : ts - t0].rearrange("p j t -> p t j"))
+        for a, t0, t1, ts, base in pieces:
+            r = raw[(a, base)]
+            nc.scalar.copy(grouped[a][:, ts:t1, :], r[:, :, ts - base : t1 - base].rearrange("p j t -> p t j"))
+            nc.vector.tensor_copy(grouped[a][:, t0:ts, :], r[:, :, t0 - base : ts - base].rearrange("p j t -> p t j"))
             nc.vector.quantize_mx(
                 out=token_words[a][:, t0:t1].bitcast(FP8X4),
                 scales=token_bytes[4 * a : P, t0:t1],
@@ -103,8 +105,6 @@ def tile_routed_moe_kernel(tc, xT, w_words, w_scales, b, gate, offs, out):
                     )
                 y = keep.tile([P, C], F32, name=f"y{e}_{c}")
                 nc.scalar.activation(y[:], acc[:], RELU, bias=bias[:, c, e : e + 1])
-                z = keep.tile([P, C], F32, name=f"z{e}_{c}")
-                nc.gpsimd.tensor_tensor(z[:], y[:], gate_rows[:, cols], MULT)
-                nc.vector.tensor_copy(windows[c][:].indirect(offsets[:, e * C // 16 : (e + 1) * C // 16]), z[:])
+                nc.vector.tensor_tensor(windows[c][:].indirect(offsets[:, e * C // 16 : (e + 1) * C // 16]), y[:], gate_rows[:, cols], MULT)
                 if e == E - 1:
                     nc.sync.dma_start(out[c * P : (c + 1) * P, :], windows[c][:])

@@ -37,43 +37,45 @@ def tile_routed_moe_kernel(tc, xT, w_words, w_scales, b, gate, offs, out):
         nc.vector.memset(w_bytes[:].rearrange("p a n -> p (a n)").bitcast(I32), 0)
         bias = keep.tile([P, BLOCKS, E], F32, name="bias")
 
+        offsets = keep.tile([P, T // 16], U16, name="offsets")
         x_rows = xT.rearrange("(a p j) t -> a p j t", p=P, j=PACK)
         raw = {}
-        for a, t0, t1 in [(0, 0, 256), (0, 256, 512), (1, 0, 512), (2, 0, 384), (2, 384, 512)]:
+        for a, t0, t1 in [(0, 0, 512), (1, 0, 512), (2, 0, 384), (2, 384, 512)]:
             r = keep.tile([P, PACK, t1 - t0], F32, name=f"raw{a}_{t0}")
             nc.sync.dma_start(r[:], x_rows[a, :, :, t0:t1])
             raw[(a, t0)] = r
-        pieces = [(0, 0, 256, 64, 0), (0, 256, 512, 320, 256), (1, 0, 512, 128, 0), (2, 0, 256, 64, 0), (2, 256, 384, 320, 0), (2, 384, 512, 448, 384)]
+            if a == 0:
+                nc.sync.dma_start(offsets[:], offs)
+        pieces = [(0, 0, 0, 96, 304, 512), (1, 0, 0, 192, 192, 512), (2, 0, 0, 96, 96, 256), (2, 0, 256, 304, 304, 384), (2, 384, 384, 384, 448, 512)]
 
-        offsets = keep.tile([P, T // 16], U16, name="offsets")
-        nc.sync.dma_start(offsets[:], offs)
+        def interleave(copy, a, base, c0, c1):
+            r = raw[(a, base)][:, :, c0 - base : c1 - base]
+            if c1 > c0:
+                copy(grouped[a][:, c0:c1, :].rearrange("p (c i) j -> p c j i", i=4), r.rearrange("p j (c i) -> p c j i", i=4))
 
+        w_codes = [keep.tile([P, PASSES, N], I32, name=f"w_codes{e}", align_bytes=64) for e in range(E)]
+        nc.sync.dma_start(w_codes[0][:], w_words[0].rearrange("a p n r -> p a (n r)").bitcast(I32))
         scale_rows = w_scales.rearrange("e a q n -> q (e a) n")
         for q in range(QUADS):
             nc.sync.dma_start(w_bytes[32 * q : 32 * q + 4, :, :].bitcast(I32), scale_rows[4 * q : 4 * q + 4, :, :].bitcast(I32))
-        w_codes = []
-        for e in range(E):
-            wc = keep.tile([P, PASSES, N], I32, name=f"w_codes{e}", align_bytes=64)
-            nc.sync.dma_start(wc[:], w_words[e].rearrange("a p n r -> p a (n r)").bitcast(I32))
-            w_codes.append(wc)
-            if e == 0:
-                nc.sync.dma_start(bias[:], b.rearrange("(c p) e -> p c e", p=P))
-                gate_rows = keep.tile([P, E * C], F32, name="gate_rows")
-                nc.sync.dma_start(gate_rows[:], gate[0:P, :])
+        nc.sync.dma_start(bias[:], b.rearrange("(c p) e -> p c e", p=P))
+        gate_rows = keep.tile([P, E * C], F32, name="gate_rows")
+        nc.sync.dma_start(gate_rows[:], gate[0:P, :])
+        nc.sync.dma_start(w_codes[1][:], w_words[1].rearrange("a p n r -> p a (n r)").bitcast(I32))
 
         grouped = [keep.tile([P, T, PACK], BF16, name=f"grouped{a}", align_bytes=64) for a in range(PASSES)]
         token_words = [keep.tile([P, T], U32, name=f"token_words{a}", align_bytes=64) for a in range(PASSES)]
-        slot_words = [keep.tile([P, E * C], U32, name=f"slot_words{a}", align_bytes=64) for a in range(PASSES)]
-        slot_bytes = keep.tile([P, E * C], U8, name="slot_bytes", align_bytes=64)
+        slot_words = [[keep.tile([P, C], U32, name=f"slot_words{e}_{a}", align_bytes=64) for a in range(PASSES)] for e in range(E)]
+        slot_bytes = [keep.tile([P, C], U8, name=f"slot_bytes{e}", align_bytes=64) for e in range(E)]
 
         def gather_words(a, e):
-            cols = slice(e * C, (e + 1) * C)
-            nc.vector.tensor_copy(slot_words[a][:, cols], token_words[a][:].indirect(offsets[:, e * C // 16 : (e + 1) * C // 16]))
+            nc.vector.tensor_copy(slot_words[e][a][:], token_words[a][:].indirect(offsets[:, e * C // 16 : (e + 1) * C // 16]))
 
-        for a, t0, t1, ts, base in pieces:
-            r = raw[(a, base)]
-            nc.scalar.copy(grouped[a][:, ts:t1, :], r[:, :, ts - base : t1 - base].rearrange("p j t -> p t j"))
-            nc.vector.tensor_copy(grouped[a][:, t0:ts, :], r[:, :, t0 - base : ts - base].rearrange("p j t -> p t j"))
+        for a, base, t0, tv, ts, t1 in pieces:
+            interleave(nc.scalar.copy, a, base, ts, t1)
+            if tv > t0:
+                nc.gpsimd.tensor_copy(grouped[a][:, t0:tv, :], raw[(a, base)][:, :, t0 - base : tv - base].rearrange("p j t -> p t j"))
+            interleave(nc.vector.tensor_copy, a, base, tv, ts)
             nc.vector.quantize_mx(
                 out=token_words[a][:, t0:t1].bitcast(FP8X4),
                 scales=token_bytes[4 * a : P, t0:t1],
@@ -82,14 +84,11 @@ def tile_routed_moe_kernel(tc, xT, w_words, w_scales, b, gate, offs, out):
             if a < PASSES - 1 and t1 == T:
                 for e in range(E):
                     gather_words(a, e)
-        for e in range(E):
-            cols = slice(e * C, (e + 1) * C)
-            nc.vector.tensor_copy(slot_bytes[:, cols], token_bytes[:].indirect(offsets[:, e * C // 16 : (e + 1) * C // 16]))
-            gather_words(PASSES - 1, e)
-
+        ys = {}
         windows = [keep.tile([P, T], F32, name=f"window{c}") for c in range(BLOCKS)]
         for e in range(E):
-            cols = slice(e * C, (e + 1) * C)
+            nc.vector.tensor_copy(slot_bytes[e][:], token_bytes[:].indirect(offsets[:, e * C // 16 : (e + 1) * C // 16]))
+            gather_words(PASSES - 1, e)
             for c in range(BLOCKS):
                 acc = psum.tile([P, C], F32, name=f"acc{e}_{c}")
                 feats = slice(c * P, (c + 1) * P)
@@ -98,13 +97,16 @@ def tile_routed_moe_kernel(tc, xT, w_words, w_scales, b, gate, offs, out):
                         out=acc[:],
                         lhsT=w_codes[e][:, a, feats].bitcast(FP8X4),
                         lhsT_scale=w_bytes[:, e * PASSES + a, feats],
-                        rhs=slot_words[a][:, cols].bitcast(FP8X4),
-                        rhs_scale=slot_bytes[4 * a : P, cols],
+                        rhs=slot_words[e][a][:].bitcast(FP8X4),
+                        rhs_scale=slot_bytes[e][4 * a : P, :],
                         start=(a == 0),
                         stop=(a == PASSES - 1),
                     )
                 y = keep.tile([P, C], F32, name=f"y{e}_{c}")
                 nc.scalar.activation(y[:], acc[:], RELU, bias=bias[:, c, e : e + 1])
-                nc.vector.tensor_tensor(windows[c][:].indirect(offsets[:, e * C // 16 : (e + 1) * C // 16]), y[:], gate_rows[:, cols], MULT)
+                ys[e, c] = y
+        for e in range(E):
+            for c in range(BLOCKS):
+                nc.vector.tensor_tensor(windows[c][:].indirect(offsets[:, e * C // 16 : (e + 1) * C // 16]), ys[e, c][:], gate_rows[:, e * C : (e + 1) * C], MULT)
                 if e == E - 1:
                     nc.sync.dma_start(out[c * P : (c + 1) * P, :], windows[c][:])

@@ -33,20 +33,21 @@ def tile_routed_moe_kernel(tc, xT, w_words, w_scales, b, gate, offs, out):
 
         token_bytes = keep.tile([P, T], U8, name="token_bytes", align_bytes=64)
         nc.gpsimd.memset(token_bytes[:], 0)
-        w_bytes = keep.tile([P, E * PASSES, N], U8, name="w_bytes", align_bytes=64)
-        nc.vector.memset(w_bytes[:].rearrange("p a n -> p (a n)").bitcast(I32), 0)
+        w_bytes = [keep.tile([P, N], U8, name=f"w_bytes{e}", align_bytes=64) for e in range(E)]
+        for e in range(E):
+            nc.vector.memset(w_bytes[e][:].bitcast(I32), 0)
         bias = keep.tile([P, BLOCKS, E], F32, name="bias")
 
         offsets = keep.tile([P, T // 16], U16, name="offsets")
         x_rows = xT.rearrange("(a p j) t -> a p j t", p=P, j=PACK)
         raw = {}
-        for a, t0, t1 in [(0, 0, 512), (1, 0, 512), (2, 0, 384), (2, 384, 512)]:
+        for a, t0, t1 in [(0, 0, 512), (1, 0, 512), (2, 0, 512)]:
             r = keep.tile([P, PACK, t1 - t0], F32, name=f"raw{a}_{t0}")
             nc.sync.dma_start(r[:], x_rows[a, :, :, t0:t1])
             raw[(a, t0)] = r
             if a == 0:
                 nc.sync.dma_start(offsets[:], offs)
-        pieces = [(0, 0, 0, 96, 304, 512), (1, 0, 0, 192, 192, 512), (2, 0, 0, 96, 96, 256), (2, 0, 256, 304, 304, 384), (2, 384, 384, 384, 448, 512)]
+        pieces = [(0, 0, 0, 64, 288, 512), (1, 0, 0, 160, 256, 512), (2, 0, 0, 112, 112, 256), (2, 0, 256, 336, 400, 512)]
 
         def interleave(copy, a, base, c0, c1):
             r = raw[(a, base)][:, :, c0 - base : c1 - base]
@@ -54,14 +55,22 @@ def tile_routed_moe_kernel(tc, xT, w_words, w_scales, b, gate, offs, out):
                 copy(grouped[a][:, c0:c1, :].rearrange("p (c i) j -> p c j i", i=4), r.rearrange("p j (c i) -> p c j i", i=4))
 
         w_codes = [keep.tile([P, PASSES, N], I32, name=f"w_codes{e}", align_bytes=64) for e in range(E)]
-        nc.sync.dma_start(w_codes[0][:], w_words[0].rearrange("a p n r -> p a (n r)").bitcast(I32))
-        scale_rows = w_scales.rearrange("e a q n -> q (e a) n")
-        for q in range(QUADS):
-            nc.sync.dma_start(w_bytes[32 * q : 32 * q + 4, :, :].bitcast(I32), scale_rows[4 * q : 4 * q + 4, :, :].bitcast(I32))
+        scale_rows = w_scales.rearrange("e a q n -> (e a) q n")
+
+        def load_w_scales(e):
+            for q in range(QUADS):
+                nc.sync.dma_start(w_bytes[e][32 * q : 32 * q + 16, :].bitcast(I32), scale_rows[2 * e : 2 * e + 4, 4 * q : 4 * q + 4, :].bitcast(I32))
+
+        def load_w_codes(e):
+            nc.sync.dma_start(w_codes[e][:], w_words[e].rearrange("a p n r -> p a (n r)").bitcast(I32))
+
+        load_w_scales(0)
+        load_w_codes(0)
         nc.sync.dma_start(bias[:], b.rearrange("(c p) e -> p c e", p=P))
         gate_rows = keep.tile([P, E * C], F32, name="gate_rows")
         nc.sync.dma_start(gate_rows[:], gate[0:P, :])
-        nc.sync.dma_start(w_codes[1][:], w_words[1].rearrange("a p n r -> p a (n r)").bitcast(I32))
+        load_w_scales(1)
+        load_w_codes(1)
 
         grouped = [keep.tile([P, T, PACK], BF16, name=f"grouped{a}", align_bytes=64) for a in range(PASSES)]
         token_words = [keep.tile([P, T], U32, name=f"token_words{a}", align_bytes=64) for a in range(PASSES)]
@@ -96,7 +105,7 @@ def tile_routed_moe_kernel(tc, xT, w_words, w_scales, b, gate, offs, out):
                     nc.tensor.matmul_mx(
                         out=acc[:],
                         lhsT=w_codes[e][:, a, feats].bitcast(FP8X4),
-                        lhsT_scale=w_bytes[:, e * PASSES + a, feats],
+                        lhsT_scale=w_bytes[e][4 * (a + e) : P, feats],
                         rhs=slot_words[e][a][:].bitcast(FP8X4),
                         rhs_scale=slot_bytes[e][4 * a : P, :],
                         start=(a == 0),

@@ -47,7 +47,7 @@ def tile_routed_moe_kernel(tc, xT, w_words, w_scales, b, gate, offs, out):
             raw[(a, t0)] = r
             if a == 0:
                 nc.sync.dma_start(offsets[:], offs)
-        pieces = [(0, 0, 0, 64, 288, 512), (1, 0, 0, 160, 256, 512), (2, 0, 0, 112, 112, 256), (2, 0, 256, 336, 400, 512)]
+        pieces = [(0, 0, 0, 0, 288, 512), (1, 0, 0, 208, 208, 512), (2, 0, 0, 112, 112, 256), (2, 0, 256, 344, 344, 512)]
 
         def interleave(copy, a, base, c0, c1):
             r = raw[(a, base)][:, :, c0 - base : c1 - base]

from contextlib import ExitStack

import concourse.mybir as mybir

K, T, E, C, N = 1536, 512, 2, 256, 512
P = 128
PACK = 4
K_PASS = P * PACK
PASSES = K // K_PASS
BLOCKS = N // P
QUADS = 4

FLOPS = 2 * K * E * C * N
BYTES = 4 * K * T + E * K * N + E * (K // 32) * N + 4 * N * E + 4 * E * C + 2 * E * C + 4 * N * T

F32 = mybir.dt.float32
BF16 = mybir.dt.bfloat16
I32 = mybir.dt.int32
U32 = mybir.dt.uint32
U16 = mybir.dt.uint16
U8 = mybir.dt.uint8
FP8X4 = mybir.dt.float8_e4m3fn_x4
COPY = mybir.ActivationFunctionType.Copy
RELU = mybir.ActivationFunctionType.Relu
MULT = mybir.AluOpType.mult


def tile_routed_moe_kernel(tc, xT, w_words, w_scales, b, gate, offs, out):
    nc = tc.nc
    with ExitStack() as ctx:
        keep = ctx.enter_context(tc.tile_pool(name="keep", bufs=1))
        psum = ctx.enter_context(tc.psum_pool(name="psum", bufs=1))

        token_bytes = keep.tile([P, T], U8, name="token_bytes", align_bytes=64)
        nc.gpsimd.memset(token_bytes[:], 0)
        w_bytes = [keep.tile([P, N], U8, name=f"w_bytes{e}", align_bytes=64) for e in range(E)]
        for e in range(E):
            nc.vector.memset(w_bytes[e][:].bitcast(I32), 0)
        bias = keep.tile([P, BLOCKS, E], F32, name="bias")

        offsets = keep.tile([P, T // 16], U16, name="offsets")
        x_rows = xT.rearrange("(a p j) t -> a p j t", p=P, j=PACK)
        raw = {}
        for a, t0, t1 in [(0, 0, 512), (1, 0, 512), (2, 0, 512)]:
            r = keep.tile([P, PACK, t1 - t0], F32, name=f"raw{a}_{t0}")
            nc.sync.dma_start(r[:], x_rows[a, :, :, t0:t1])
            raw[(a, t0)] = r
            if a == 0:
                nc.sync.dma_start(offsets[:], offs)
        pieces = [(0, 0, 0, 0, 288, 512), (1, 0, 0, 208, 208, 512), (2, 0, 0, 112, 112, 256), (2, 0, 256, 344, 344, 512)]

        def interleave(copy, a, base, c0, c1):
            r = raw[(a, base)][:, :, c0 - base : c1 - base]
            if c1 > c0:
                copy(grouped[a][:, c0:c1, :].rearrange("p (c i) j -> p c j i", i=4), r.rearrange("p j (c i) -> p c j i", i=4))

        w_codes = [keep.tile([P, PASSES, N], I32, name=f"w_codes{e}", align_bytes=64) for e in range(E)]
        scale_rows = w_scales.rearrange("e a q n -> (e a) q n")

        def load_w_scales(e):
            for q in range(QUADS):
                nc.sync.dma_start(w_bytes[e][32 * q : 32 * q + 16, :].bitcast(I32), scale_rows[2 * e : 2 * e + 4, 4 * q : 4 * q + 4, :].bitcast(I32))

        def load_w_codes(e):
            nc.sync.dma_start(w_codes[e][:], w_words[e].rearrange("a p n r -> p a (n r)").bitcast(I32))

        load_w_scales(0)
        load_w_codes(0)
        nc.sync.dma_start(bias[:], b.rearrange("(c p) e -> p c e", p=P))
        gate_rows = keep.tile([P, E * C], F32, name="gate_rows")
        nc.sync.dma_start(gate_rows[:], gate[0:P, :])
        load_w_scales(1)
        load_w_codes(1)

        grouped = [keep.tile([P, T, PACK], BF16, name=f"grouped{a}", align_bytes=64) for a in range(PASSES)]
        token_words = [keep.tile([P, T], U32, name=f"token_words{a}", align_bytes=64) for a in range(PASSES)]
        slot_words = [[keep.tile([P, C], U32, name=f"slot_words{e}_{a}", align_bytes=64) for a in range(PASSES)] for e in range(E)]
        slot_bytes = [keep.tile([P, C], U8, name=f"slot_bytes{e}", align_bytes=64) for e in range(E)]

        def gather_words(a, e):
            nc.vector.tensor_copy(slot_words[e][a][:], token_words[a][:].indirect(offsets[:, e * C // 16 : (e + 1) * C // 16]))

        for a, base, t0, tv, ts, t1 in pieces:
            interleave(nc.scalar.copy, a, base, ts, t1)
            if tv > t0:
                nc.gpsimd.tensor_copy(grouped[a][:, t0:tv, :], raw[(a, base)][:, :, t0 - base : tv - base].rearrange("p j t -> p t j"))
            interleave(nc.vector.tensor_copy, a, base, tv, ts)
            nc.vector.quantize_mx(
                out=token_words[a][:, t0:t1].bitcast(FP8X4),
                scales=token_bytes[4 * a : P, t0:t1],
                in_=grouped[a][:, t0:t1, :].rearrange("p t j -> p (t j)"),
            )
            if a < PASSES - 1 and t1 == T:
                for e in range(E):
                    gather_words(a, e)
        ys = {}
        windows = [keep.tile([P, T], F32, name=f"window{c}") for c in range(BLOCKS)]
        for e in range(E):
            nc.vector.tensor_copy(slot_bytes[e][:], token_bytes[:].indirect(offsets[:, e * C // 16 : (e + 1) * C // 16]))
            gather_words(PASSES - 1, e)
            for c in range(BLOCKS):
                acc = psum.tile([P, C], F32, name=f"acc{e}_{c}")
                feats = slice(c * P, (c + 1) * P)
                for a in range(PASSES):
                    nc.tensor.matmul_mx(
                        out=acc[:],
                        lhsT=w_codes[e][:, a, feats].bitcast(FP8X4),
                        lhsT_scale=w_bytes[e][4 * (a + e) : P, feats],
                        rhs=slot_words[e][a][:].bitcast(FP8X4),
                        rhs_scale=slot_bytes[e][4 * a : P, :],
                        start=(a == 0),
                        stop=(a == PASSES - 1),
                    )
                y = keep.tile([P, C], F32, name=f"y{e}_{c}")
                nc.scalar.activation(y[:], acc[:], RELU, bias=bias[:, c, e : e + 1])
                ys[e, c] = y
        for e in range(E):
            for c in range(BLOCKS):
                nc.vector.tensor_tensor(windows[c][:].indirect(offsets[:, e * C // 16 : (e + 1) * C // 16]), ys[e, c][:], gate_rows[:, e * C : (e + 1) * C], MULT)
                if e == E - 1:
                    nc.sync.dma_start(out[c * P : (c + 1) * P, :], windows[c][:])
